import numpy as np, ml_dtypes
CORES = [24,25,26,27,28,29,30,31]
N = 8
import mx_ref
BF = ml_dtypes.bfloat16
def entries(a):
    return np.ascontiguousarray(a.T).reshape(-1)
def table(e):
    return np.ascontiguousarray(np.reshape(e, (-1, 16)).T).astype(np.int32)
def cols(t, e):
    v = np.concatenate([t.reshape(128, -1, 4), np.zeros((128, 1, 4), BF)], axis=1)
    return np.ascontiguousarray(v[:, e]).reshape(128, -1)
def tile(rs):
    return np.stack(rs, axis=2).reshape(128, -1).astype(BF)
def f(rng, *shape):
    return mx_ref.flush((rng.standard_normal(shape, dtype=np.float32) * np.exp2(rng.integers(-2, 3, shape[:-1] + (1,)))).astype(BF))
def wide(rng, *shape, cols=0):
    v = rng.standard_normal(shape, dtype=np.float32) * np.exp2(rng.integers(-12, 13, shape)).astype(np.float32)
    if cols: v *= np.repeat(np.exp2(rng.integers(-cols, cols + 1, shape[:-2] + (1, shape[-1] // 4))) * (rng.random(shape[:-2] + (1, shape[-1] // 4)) > 0.0625), 4, axis=-1).astype(np.float32)
    return mx_ref.flush(v.astype(BF))
T, E, EC, CAPP = 256, 4, 128, 48
def lists(rng, case=""):
    sn, so = np.full((N, N, CAPP), -1), np.full((N, E, EC), -1)
    lone = rng.integers(0, N)
    for d in range(N):
        a = rng.integers(0, E)
        n = rng.integers(CAPP // 4, CAPP + 1, N)
        if case == "full": n[:] = CAPP
        if case == "empty": n[(d + 1) % N] = 0
        if case == "empty" and d == lone: n[np.arange(N) != d] = 0
        used = np.concatenate([s * CAPP + (np.arange(n[s]) if case == "sorted" else rng.permutation(CAPP)[:n[s]]) for s in range(N)])
        if case == "one": used = rng.permutation(N * CAPP)[:EC + rng.integers(E - 1, 8 * E - 7)]
        if case != "sorted": used = rng.permutation(used)
        if case == "empty": used = used[:(E - 1) * EC]
        key = rng.random((E, EC)) * np.exp2(rng.integers(-1, 2, (E, 1)))
        if case in ("full", "one"): key[a] = -1
        if case == "empty": key[a] = 9
        who = np.argsort(key.reshape(-1))[:len(used)] // EC
        if case == "sorted": who = np.sort(who)
        for m in range(E):
            k = used[who == m]; so[d, m, :len(k)] = k
        sn[used // CAPP, d, used % CAPP] = rng.integers(0, T, len(used))
        if case == "sorted":
            for s in range(N): sn[s, d, :n[s]] = np.sort(sn[s, d, :n[s]])
    return {"sn": np.stack([table(q) for q in sn]), "so": np.stack([table(q) for q in so])}
def setup_inputs(rng):
    return {"x": f(rng, N, 128, 4 * T), "w": f(rng, N, 128, 2048 * E), "v": f(rng, N, 128, 512 * E), **lists(rng)}
def setup_inputs_full(rng):
    return {**setup_inputs(rng), **lists(rng, "full")}
def setup_inputs_one(rng):
    return {**setup_inputs(rng), **lists(rng, "one")}
def setup_inputs_empty(rng):
    return {**setup_inputs(rng), **lists(rng, "empty")}
def setup_inputs_sorted(rng):
    return {**setup_inputs(rng), **lists(rng, "sorted")}
def setup_inputs_spread(rng):
    d = setup_inputs(rng); d["x"] = wide(rng, N, 128, 4 * T, cols=6); return d
def check_inputs(d):
    b = []
    for r in range(N):
        c, e = entries(d["sn"][r]), entries(d["so"][r]).reshape(E, EC)
        if c.min() < -1 or c.max() >= T: b.append("sn")
        got = np.concatenate([entries(d["sn"][s])[r * CAPP:(r + 1) * CAPP] for s in range(N)])
        if e.min() < -1 or ((e[:, 1:] >= 0) & (e[:, :-1] < 0)).any() or np.sort(e[e >= 0]).tolist() != np.flatnonzero(got >= 0).tolist(): b.append("so")
    return b
def reference(x, w, v, sn, so):
    y = np.zeros((N, 128, E * EC), np.float32)
    for r in range(N):
        arrived = np.concatenate([cols(x[s], entries(sn[s])[r * CAPP:(r + 1) * CAPP]) for s in range(N)], axis=1)
        e = entries(so[r])
        for m in range(E):
            k = e[EC * m:EC * m + EC]
            t = mx_ref.quantize(cols(arrived, k))
            R = []
            for i in range(4):
                W = mx_ref.quantize(np.ascontiguousarray(w[r][:, 2048 * m + 512 * i:2048 * m + 512 * i + 512]))
                R.append(np.maximum(mx_ref.matmul(W, t), np.float32(0)) * np.float32(0.05))
            z = mx_ref.matmul(mx_ref.quantize(np.ascontiguousarray(v[r][:, 512 * m:512 * m + 512])), mx_ref.quantize(tile(R)))
            y[r][:, EC * m:EC * m + EC] = np.where(k >= 0, z, np.float32(0))
    return {"y": y}

@@ -1,0 +1,230 @@
+from concourse.bass import DstId, RemoteDMATransfer
+from concourse.mybir import dt, AluOpType, ActivationFunctionType
+
+E, EC, CAPP, NR, TOK = 4, 128, 48, 8, 256
+F8 = "float8_e4m3fn_x4"
+WIN = EC + NR * CAPP
+SCRATCH = {
+    "snt": ("sbuf", [128, 24], "int32"),
+    "sot": ("sbuf", [128, 32], "int32"),
+    "offs": ("sbuf", [128, 32], "uint16"),
+    "offt": ("sbuf", [128, 32], "uint16"),
+    "xt": ("sbuf", [128, 4 * TOK], "bfloat16"),
+    "xq": ("sbuf", [128, TOK], F8),
+    "xs": ("sbuf", [128, TOK], "uint8"),
+    "slotq": ("sbuf", [128, (NR - 1) * CAPP], F8),
+    "slots": ("sbuf", [128, (NR - 1) * CAPP], "uint8"),
+    "zt": ("sbuf", [128, 4 * EC], "bfloat16"),
+    "landq": ("sbuf", [128, WIN], F8),
+    "lands": ("sbuf", [128, WIN], "uint8"),
+    "tokq": ("sbuf", [128, E * EC], F8),
+    "toks": ("sbuf", [128, E * EC], "uint8"),
+    "wt": ("sbuf", [128, 2048 * E], "bfloat16"),
+    "wq": ("sbuf", [128, 512 * E], F8),
+    "ws": ("sbuf", [128, 512 * E], "uint8"),
+    "vt": ("sbuf", [128, 512 * E], "bfloat16"),
+    "vq": ("sbuf", [128, 128 * E], F8),
+    "vs": ("sbuf", [128, 128 * E], "uint8"),
+    "ht": ("sbuf", [128, 4 * EC * E], "bfloat16"),
+    "hq": ("sbuf", [128, EC * E], F8),
+    "hs": ("sbuf", [128, EC * E], "uint8"),
+    "yt": ("sbuf", [128, EC * E], "float32"),
+}
+for _i in range(8):
+    SCRATCH["ps%d" % _i] = ("psum", [128, 512], "float32")
+SEMAPHORES = ["snl", "xl", "sol", "vl", "zm", "zq", "cv", "cvo", "cvt", "xqd", "pc", "psc", "oc", "osc",
+              "arrc", "arrs", "loc", "gate", "vqd", "yd"]
+for _m in range(E):
+    SEMAPHORES += ["wl%d" % _m, "wqd%d" % _m, "pkc%d" % _m, "pks%d" % _m, "hqd%d" % _m, "mv%d" % _m, "ye%d" % _m,
+                   "evv%d" % _m, "evs%d" % _m]
+    SEMAPHORES += ["mm%d_%d" % (_m, _b) for _b in range(4)]
+
+
+def rank_program(g, core, T, topo):
+    r = T.rank_of(core)
+    if r is None:
+        return
+    S, V, A, P = T.sem, g.vector, g.scalar, g.tensor
+    COPY, RELU = ActivationFunctionType.Copy, ActivationFunctionType.Relu
+
+    def u32(ap):
+        return ap.bitcast(dt.uint32)
+
+    g.sync.dma_start(T.xt[:, :], T.x[:, :]).then_inc(S.xl, 16)
+    for k in range(8):
+        q = g.sync if k >= 5 else A
+        q.dma_start(T.snt[16 * k:16 * k + 16, :], T.sn[:, :]).then_inc(S.snl, 16)
+
+    def load_w(m):
+        g.sync.dma_start(T.wt[:, 2048 * m:2048 * m + 2048], T.w[:, 2048 * m:2048 * m + 2048]).then_inc(S["wl%d" % m], 16)
+
+    load_w(0)
+    load_w(1)
+    g.sync.wait_ge(S.gate, 1)
+    g.sync.dma_start(T.vt[:, :], T.v[:, :]).then_inc(S.vl, 16)
+    load_w(2)
+    load_w(3)
+
+    V.memset(T.zt[:, :], 0.0).then_inc(S.zm, 1)
+    V.wait_ge(S.zm, 1)
+    V.quantize_mx(T.landq[:, 0:EC], T.lands[:, 0:EC], T.zt[:, :]).then_inc(S.zq, 1)
+    K = CAPP // 16
+    ncv = 0
+    V.wait_ge(S.snl, 128)
+    if r > 0:
+        V.tensor_copy(T.offs[:, 0:K * r], T.snt[:, 0:K * r]).then_inc(S.cv, 1)
+        ncv += 1
+    if r < NR - 1:
+        V.tensor_copy(T.offs[:, K * r:K * (NR - 1)], T.snt[:, K * (r + 1):K * NR]).then_inc(S.cv, 1)
+        ncv += 1
+    V.wait_ge(S.xl, 16)
+    V.quantize_mx(T.xq[:, :], T.xs[:, :], T.xt[:, :]).then_inc(S.xqd, 1)
+    V.wait_ge(S.cv, ncv)
+    V.wait_ge(S.xqd, 1)
+    n7 = K * (NR - 1)
+    V.tensor_copy(u32(T.slotq[:, :]), u32(T.xq[:, :]).indirect(T.offs[:, 0:n7])).then_inc(S.pc, 1)
+    A.wait_ge(S.cv, ncv)
+    A.wait_ge(S.xqd, 1)
+    A.activation(T.slots[:, :], T.xs[:, :].indirect(T.offs[:, 0:n7]), COPY).then_inc(S.psc, 1)
+    o0 = n7 + n7 % 2
+    own = EC + CAPP * r
+    V.tensor_copy(T.offs[:, o0:o0 + K], T.snt[:, K * r:K * r + K]).then_inc(S.cvo, 1)
+    V.wait_ge(S.cvo, 1)
+    V.tensor_copy(u32(T.landq[:, own:own + CAPP]), u32(T.xq[:, :]).indirect(T.offs[:, o0:o0 + K])).then_inc(S.oc, 1)
+    for k in range(8):
+        A.dma_start(T.sot[16 * k:16 * k + 16, :], T.so[:, :]).then_inc(S.sol, 16)
+    A.wait_ge(S.cvo, 1)
+    A.activation(T.lands[:, own:own + CAPP], T.xs[:, :].indirect(T.offs[:, o0:o0 + K]), COPY).then_inc(S.osc, 1)
+
+    far, near, plan = 0, 0, []
+    for i in range(1, NR):
+        d = (r + i) % NR
+        dst = T.cores[d]
+        e = topo.engines(core, dst)
+        if topo.die(dst) != topo.die(core):
+            use = e[0::2][2 * far:2 * far + 2]
+            far += 1
+        else:
+            use = e[1::2][2 * near:2 * near + 2]
+            near += 1
+        rid, pid, _ = topo.addr(dst)
+        plan.append((d if d < r else d - 1, DstId(rid=rid, pnc=pid), sum(1 << k for k in use)))
+
+    def send(codes):
+        ts = []
+        for j, did, mask in plan:
+            if codes:
+                src = T.slotq[:, CAPP * j:CAPP * j + CAPP].bitcast(dt.uint8)
+                dst = T.landq[:, own:own + CAPP].bitcast(dt.uint8)
+            else:
+                src = T.slots[:, CAPP * j:CAPP * j + CAPP]
+                dst = T.lands[:, own:own + CAPP]
+            ts.append(RemoteDMATransfer(dst_ids=[did], dma_engine_mask=mask, remote_sem=S.arrc if codes else S.arrs, src=src, dst=dst))
+        g.remote_dma_fused(ts, local_sem=S.loc)
+
+    narr = 2 * (NR - 1)
+    g.wait_ge(S.pc, 1)
+    send(True)
+    g.wait_ge(S.psc, 1)
+    send(False)
+    g.sem_inc(S.gate, 1)
+    g.wait_ge(S.loc, 2 * narr)
+
+    def quant_w(m):
+        V.wait_ge(S["wl%d" % m], 16)
+        V.quantize_mx(T.wq[:, 512 * m:512 * m + 512], T.ws[:, 512 * m:512 * m + 512], T.wt[:, 2048 * m:2048 * m + 2048]).then_inc(S["wqd%d" % m], 1)
+
+    quant_w(0)
+    V.wait_ge(S.sol, 128)
+    V.tensor_scalar(T.offt[:, :], T.sot[:, :], EC, None, AluOpType.add).then_inc(S.cvt, 1)
+    quant_w(1)
+    V.wait_ge(S.vl, 16)
+    V.quantize_mx(T.vq[:, :], T.vs[:, :], T.vt[:, :]).then_inc(S.vqd, 1)
+    quant_w(2)
+
+    def bank(m, b):
+        return T["ps%d" % (4 * (m % 2) + b)][:, 0:EC]
+
+    def pick_codes(m):
+        if m == 0:
+            V.wait_ge(S.cvt, 1)
+            V.wait_ge(S.zq, 1)
+            V.wait_ge(S.oc, 1)
+            V.wait_ge(S.arrc, narr)
+        V.tensor_copy(u32(T.tokq[:, EC * m:EC * m + EC]), u32(T.landq[:, :]).indirect(T.offt[:, 8 * m:8 * m + 8])).then_inc(S["pkc%d" % m], 1)
+
+    def pick_scales(m):
+        if m == 0:
+            A.wait_ge(S.cvt, 1)
+            A.wait_ge(S.zq, 1)
+            A.wait_ge(S.osc, 1)
+            A.wait_ge(S.arrs, narr)
+        A.activation(T.toks[:, EC * m:EC * m + EC], T.lands[:, :].indirect(T.offt[:, 8 * m:8 * m + 8]), COPY).then_inc(S["pks%d" % m], 1)
+
+    def h_out(m, b):
+        return T.ht[:, 512 * m + b:512 * m + 512:4]
+
+    def evac_v(m, b):
+        V.wait_ge(S["mm%d_%d" % (m, b)], 1)
+        V.tensor_scalar(h_out(m, b), bank(m, b), 0.0, 0.05, AluOpType.max, AluOpType.mult).then_inc(S["evv%d" % m], 1)
+
+    def evac_s(m, b):
+        A.wait_ge(S["mm%d_%d" % (m, b)], 1)
+        A.activation(h_out(m, b), bank(m, b), RELU, scale=0.05).then_inc(S["evs%d" % m], 1)
+
+    def quant_h(m):
+        V.wait_ge(S["evv%d" % m], 2)
+        V.wait_ge(S["evs%d" % m], 2)
+        V.quantize_mx(T.hq[:, EC * m:EC * m + EC], T.hs[:, EC * m:EC * m + EC], T.ht[:, 512 * m:512 * m + 512]).then_inc(S["hqd%d" % m], 1)
+
+    def y_out(m):
+        A.wait_ge(S["mv%d" % m], 1)
+        A.activation(T.yt[:, EC * m:EC * m + EC], bank(m, 3), COPY).then_inc(S["ye%d" % m], 1)
+        g.sync.wait_ge(S["ye%d" % m], 1)
+        g.sync.dma_start(T.y[:, EC * m:EC * m + EC], T.yt[:, EC * m:EC * m + EC]).then_inc(S.yd, 16)
+
+    def mm_w(m):
+        P.wait_ge(S["wqd%d" % m], 1)
+        P.wait_ge(S["pkc%d" % m], 1)
+        P.wait_ge(S["pks%d" % m], 1)
+        for b in range(4):
+            if m >= 2 and b == 3:
+                P.wait_ge(S["ye%d" % (m - 2)], 1)
+            c = 512 * m + 128 * b
+            P.matmul_mx(bank(m, b), T.wq[:, c:c + 128], T.ws[:, c:c + 128], T.tokq[:, EC * m:EC * m + EC],
+                        T.toks[:, EC * m:EC * m + EC], True, True).then_inc(S["mm%d_%d" % (m, b)], 1)
+
+    def mm_v(m):
+        if m == 0:
+            P.wait_ge(S.vqd, 1)
+        P.wait_ge(S["hqd%d" % m], 1)
+        P.matmul_mx(bank(m, 3), T.vq[:, 128 * m:128 * m + 128], T.vs[:, 128 * m:128 * m + 128], T.hq[:, EC * m:EC * m + EC],
+                    T.hs[:, EC * m:EC * m + EC], True, True).then_inc(S["mv%d" % m], 1)
+
+    mm_w(0)
+    mm_w(1)
+    mm_v(0)
+    mm_w(2)
+    mm_v(1)
+    mm_w(3)
+    mm_v(2)
+    mm_v(3)
+    pick_codes(0)
+    pick_codes(1)
+    for m in range(E):
+        evac_v(m, 0)
+        evac_v(m, 2)
+        if m + 2 < E:
+            pick_codes(m + 2)
+        quant_h(m)
+        if m == 0:
+            quant_w(3)
+    pick_scales(0)
+    pick_scales(1)
+    for m in range(E):
+        evac_s(m, 1)
+        evac_s(m, 3)
+        if m + 2 < E:
+            pick_scales(m + 2)
+        y_out(m)
+    g.sync.wait_ge(S.yd, 16 * E)

@@ -4,6 +4,7 @@ from concourse.mybir import dt, AluOpType, ActivationFunctionType
 E, EC, CAPP, NR, TOK = 4, 128, 48, 8, 256
 F8 = "float8_e4m3fn_x4"
 WIN = EC + NR * CAPP
+ON_SCALAR = ((1, 3), (1, 3), (1, 3), (0, 1, 3))
 SCRATCH = {
     "snt": ("sbuf", [128, 24], "int32"),
     "sot": ("sbuf", [128, 32], "int32"),
@@ -33,11 +34,11 @@ SCRATCH = {
 for _i in range(8):
     SCRATCH["ps%d" % _i] = ("psum", [128, 512], "float32")
 SEMAPHORES = ["snl", "xl", "sol", "vl", "zm", "zq", "cv", "cvo", "cvt", "xqd", "pc", "psc", "oc", "osc",
-              "arrc", "arrs", "loc", "gate", "vqd", "yd"]
+              "arrc", "arrs", "loc", "vqd", "yd", "wl3b", "wqd3b"]
 for _m in range(E):
-    SEMAPHORES += ["wl%d" % _m, "wqd%d" % _m, "pkc%d" % _m, "pks%d" % _m, "hqd%d" % _m, "mv%d" % _m, "ye%d" % _m,
-                   "evv%d" % _m, "evs%d" % _m]
+    SEMAPHORES += ["wl%d" % _m, "wqd%d" % _m, "pkc%d" % _m, "pks%d" % _m, "hqd%d" % _m, "mv%d" % _m, "ye%d" % _m]
     SEMAPHORES += ["mm%d_%d" % (_m, _b) for _b in range(4)]
+    SEMAPHORES += ["ev%d_%d" % (_m, _b) for _b in range(4)]
 
 
 def rank_program(g, core, T, topo):
@@ -50,20 +51,21 @@ def rank_program(g, core, T, topo):
     def u32(ap):
         return ap.bitcast(dt.uint32)
 
+    def load_w(tag, a, b):
+        g.sync.dma_start(T.wt[:, 512 * a:512 * b], T.w[:, 512 * a:512 * b]).then_inc(S["wl" + tag], 16)
+
     g.sync.dma_start(T.xt[:, :], T.x[:, :]).then_inc(S.xl, 16)
     for k in range(8):
         q = g.sync if k >= 5 else A
         q.dma_start(T.snt[16 * k:16 * k + 16, :], T.sn[:, :]).then_inc(S.snl, 16)
-
-    def load_w(m):
-        g.sync.dma_start(T.wt[:, 2048 * m:2048 * m + 2048], T.w[:, 2048 * m:2048 * m + 2048]).then_inc(S["wl%d" % m], 16)
-
-    load_w(0)
-    load_w(1)
-    g.sync.wait_ge(S.gate, 1)
-    g.sync.dma_start(T.vt[:, :], T.v[:, :]).then_inc(S.vl, 16)
-    load_w(2)
-    load_w(3)
+    load_w("0", 0, 4)
+    A.dma_start(T.vt[:, :], T.v[:, :]).then_inc(S.vl, 16)
+    load_w("1", 4, 8)
+    load_w("2", 8, 12)
+    load_w("3", 12, 14)
+    load_w("3b", 14, 16)
+    for k in range(4):
+        g.sync.dma_start(T.sot[16 * k:16 * k + 16, :], T.so[:, :]).then_inc(S.sol, 16)
 
     V.memset(T.zt[:, :], 0.0).then_inc(S.zm, 1)
     V.wait_ge(S.zm, 1)
@@ -91,7 +93,7 @@ def rank_program(g, core, T, topo):
     V.tensor_copy(T.offs[:, o0:o0 + K], T.snt[:, K * r:K * r + K]).then_inc(S.cvo, 1)
     V.wait_ge(S.cvo, 1)
     V.tensor_copy(u32(T.landq[:, own:own + CAPP]), u32(T.xq[:, :]).indirect(T.offs[:, o0:o0 + K])).then_inc(S.oc, 1)
-    for k in range(8):
+    for k in range(4, 8):
         A.dma_start(T.sot[16 * k:16 * k + 16, :], T.so[:, :]).then_inc(S.sol, 16)
     A.wait_ge(S.cvo, 1)
     A.activation(T.lands[:, own:own + CAPP], T.xs[:, :].indirect(T.offs[:, o0:o0 + K]), COPY).then_inc(S.osc, 1)
@@ -127,54 +129,36 @@ def rank_program(g, core, T, topo):
     send(True)
     g.wait_ge(S.psc, 1)
     send(False)
-    g.sem_inc(S.gate, 1)
     g.wait_ge(S.loc, 2 * narr)
 
-    def quant_w(m):
-        V.wait_ge(S["wl%d" % m], 16)
-        V.quantize_mx(T.wq[:, 512 * m:512 * m + 512], T.ws[:, 512 * m:512 * m + 512], T.wt[:, 2048 * m:2048 * m + 2048]).then_inc(S["wqd%d" % m], 1)
-
-    quant_w(0)
-    V.wait_ge(S.sol, 128)
-    V.tensor_scalar(T.offt[:, :], T.sot[:, :], EC, None, AluOpType.add).then_inc(S.cvt, 1)
-    quant_w(1)
-    V.wait_ge(S.vl, 16)
-    V.quantize_mx(T.vq[:, :], T.vs[:, :], T.vt[:, :]).then_inc(S.vqd, 1)
-    quant_w(2)
+    def quant_w(tag, a, b):
+        V.wait_ge(S["wl" + tag], 16)
+        V.quantize_mx(T.wq[:, 128 * a:128 * b], T.ws[:, 128 * a:128 * b], T.wt[:, 512 * a:512 * b]).then_inc(S["wqd" + tag], 1)
 
     def bank(m, b):
         return T["ps%d" % (4 * (m % 2) + b)][:, 0:EC]
 
     def pick_codes(m):
-        if m == 0:
-            V.wait_ge(S.cvt, 1)
-            V.wait_ge(S.zq, 1)
-            V.wait_ge(S.oc, 1)
-            V.wait_ge(S.arrc, narr)
         V.tensor_copy(u32(T.tokq[:, EC * m:EC * m + EC]), u32(T.landq[:, :]).indirect(T.offt[:, 8 * m:8 * m + 8])).then_inc(S["pkc%d" % m], 1)
 
     def pick_scales(m):
-        if m == 0:
-            A.wait_ge(S.cvt, 1)
-            A.wait_ge(S.zq, 1)
-            A.wait_ge(S.osc, 1)
-            A.wait_ge(S.arrs, narr)
         A.activation(T.toks[:, EC * m:EC * m + EC], T.lands[:, :].indirect(T.offt[:, 8 * m:8 * m + 8]), COPY).then_inc(S["pks%d" % m], 1)
 
     def h_out(m, b):
         return T.ht[:, 512 * m + b:512 * m + 512:4]
 
-    def evac_v(m, b):
-        V.wait_ge(S["mm%d_%d" % (m, b)], 1)
-        V.tensor_scalar(h_out(m, b), bank(m, b), 0.0, 0.05, AluOpType.max, AluOpType.mult).then_inc(S["evv%d" % m], 1)
-
-    def evac_s(m, b):
-        A.wait_ge(S["mm%d_%d" % (m, b)], 1)
-        A.activation(h_out(m, b), bank(m, b), RELU, scale=0.05).then_inc(S["evs%d" % m], 1)
+    def evac(m, *bs):
+        for b in bs:
+            if b in ON_SCALAR[m]:
+                A.wait_ge(S["mm%d_%d" % (m, b)], 1)
+                A.activation(h_out(m, b), bank(m, b), RELU, scale=0.05).then_inc(S["ev%d_%d" % (m, b)], 1)
+            else:
+                V.wait_ge(S["mm%d_%d" % (m, b)], 1)
+                V.tensor_scalar(h_out(m, b), bank(m, b), 0.0, 0.05, AluOpType.max, AluOpType.mult).then_inc(S["ev%d_%d" % (m, b)], 1)
 
     def quant_h(m):
-        V.wait_ge(S["evv%d" % m], 2)
-        V.wait_ge(S["evs%d" % m], 2)
+        for b in range(4):
+            V.wait_ge(S["ev%d_%d" % (m, b)], 1)
         V.quantize_mx(T.hq[:, EC * m:EC * m + EC], T.hs[:, EC * m:EC * m + EC], T.ht[:, 512 * m:512 * m + 512]).then_inc(S["hqd%d" % m], 1)
 
     def y_out(m):
@@ -183,11 +167,14 @@ def rank_program(g, core, T, topo):
         g.sync.wait_ge(S["ye%d" % m], 1)
         g.sync.dma_start(T.y[:, EC * m:EC * m + EC], T.yt[:, EC * m:EC * m + EC]).then_inc(S.yd, 16)
 
-    def mm_w(m):
-        P.wait_ge(S["wqd%d" % m], 1)
-        P.wait_ge(S["pkc%d" % m], 1)
-        P.wait_ge(S["pks%d" % m], 1)
-        for b in range(4):
+    def mm_w(m, *bs):
+        for b in bs:
+            if b == 0:
+                P.wait_ge(S["wqd%d" % m], 1)
+                P.wait_ge(S["pkc%d" % m], 1)
+                P.wait_ge(S["pks%d" % m], 1)
+            if m == 3 and b == 2:
+                P.wait_ge(S.wqd3b, 1)
             if m >= 2 and b == 3:
                 P.wait_ge(S["ye%d" % (m - 2)], 1)
             c = 512 * m + 128 * b
@@ -201,30 +188,51 @@ def rank_program(g, core, T, topo):
         P.matmul_mx(bank(m, 3), T.vq[:, 128 * m:128 * m + 128], T.vs[:, 128 * m:128 * m + 128], T.hq[:, EC * m:EC * m + EC],
                     T.hs[:, EC * m:EC * m + EC], True, True).then_inc(S["mv%d" % m], 1)
 
-    mm_w(0)
-    mm_w(1)
+    mm_w(0, 0, 1, 2, 3)
+    mm_w(1, 0, 1, 2, 3)
     mm_v(0)
-    mm_w(2)
+    mm_w(2, 0, 1, 2, 3)
     mm_v(1)
-    mm_w(3)
+    mm_w(3, 0, 1)
     mm_v(2)
+    mm_w(3, 2, 3)
     mm_v(3)
+    quant_w("0", 0, 4)
+    V.wait_ge(S.vl, 16)
+    V.quantize_mx(T.vq[:, :], T.vs[:, :], T.vt[:, :]).then_inc(S.vqd, 1)
+    quant_w("1", 4, 8)
+    V.wait_ge(S.sol, 128)
+    V.tensor_scalar(T.offt[:, :], T.sot[:, :], EC, None, AluOpType.add).then_inc(S.cvt, 1)
+    V.wait_ge(S.cvt, 1)
+    V.wait_ge(S.zq, 1)
+    V.wait_ge(S.oc, 1)
+    V.wait_ge(S.arrc, narr)
     pick_codes(0)
     pick_codes(1)
-    for m in range(E):
-        evac_v(m, 0)
-        evac_v(m, 2)
-        if m + 2 < E:
-            pick_codes(m + 2)
-        quant_h(m)
-        if m == 0:
-            quant_w(3)
+    A.wait_ge(S.cvt, 1)
+    A.wait_ge(S.zq, 1)
+    A.wait_ge(S.osc, 1)
+    A.wait_ge(S.arrs, narr)
     pick_scales(0)
     pick_scales(1)
-    for m in range(E):
-        evac_s(m, 1)
-        evac_s(m, 3)
-        if m + 2 < E:
-            pick_scales(m + 2)
-        y_out(m)
+    evac(0, 0, 1, 2, 3)
+    pick_codes(2)
+    pick_scales(2)
+    quant_h(0)
+    y_out(0)
+    quant_w("2", 8, 12)
+    evac(1, 0, 1, 2, 3)
+    pick_codes(3)
+    pick_scales(3)
+    quant_h(1)
+    y_out(1)
+    quant_w("3", 12, 14)
+    evac(2, 0, 1, 2, 3)
+    quant_h(2)
+    quant_w("3b", 14, 16)
+    evac(3, 0, 1)
+    y_out(2)
+    evac(3, 2, 3)
+    quant_h(3)
+    y_out(3)
     g.sync.wait_ge(S.yd, 16 * E)

@@ -4,7 +4,10 @@ from concourse.mybir import dt, AluOpType, ActivationFunctionType
 E, EC, CAPP, NR, TOK = 4, 128, 48, 8, 256
 F8 = "float8_e4m3fn_x4"
 WIN = EC + NR * CAPP
-ON_SCALAR = ((1, 3), (1, 3), (1, 3), (0, 1, 3))
+TENSOR = "m00 m02 m01 m12 m03 m10 m11 m13 m21 m22 v0 m20 m30 v1 m23 m32 m31 m33 v2 v3".split()
+VECTOR = "p0 p1 p2 s1 w2 e00 e12 p3 h0 w3 e11 h1 w3b e20 y1 e30 h2 e33 h3 y2".split()
+SCALAR = "s0 s2 s3 e02 e01 e03 e10 e13 e21 y0 e22 e23 e32 e31 y3".split()
+PIECES = {"0": (0, 4), "1": (4, 8), "2": (8, 12), "3": (12, 14), "3b": (14, 16)}
 SCRATCH = {
     "snt": ("sbuf", [128, 24], "int32"),
     "sot": ("sbuf", [128, 32], "int32"),
@@ -34,11 +37,8 @@ SCRATCH = {
 for _i in range(8):
     SCRATCH["ps%d" % _i] = ("psum", [128, 512], "float32")
 SEMAPHORES = ["snl", "xl", "sol", "vl", "zm", "zq", "cv", "cvo", "cvt", "xqd", "pc", "psc", "oc", "osc",
-              "arrc", "arrs", "loc", "vqd", "yd", "wl3b", "wqd3b"]
-for _m in range(E):
-    SEMAPHORES += ["wl%d" % _m, "wqd%d" % _m, "pkc%d" % _m, "pks%d" % _m, "hqd%d" % _m, "mv%d" % _m, "ye%d" % _m]
-    SEMAPHORES += ["mm%d_%d" % (_m, _b) for _b in range(4)]
-    SEMAPHORES += ["ev%d_%d" % (_m, _b) for _b in range(4)]
+              "arrc", "arrs", "loc", "vqd", "yd"]
+SEMAPHORES += ["wl" + _t for _t in PIECES] + ["wqd" + _t for _t in PIECES] + sorted(set(TENSOR + VECTOR + SCALAR) - {"w2", "w3", "w3b"})
 
 
 def rank_program(g, core, T, topo):
@@ -51,21 +51,25 @@ def rank_program(g, core, T, topo):
     def u32(ap):
         return ap.bitcast(dt.uint32)
 
-    def load_w(tag, a, b):
+    def load_w(tag):
+        a, b = PIECES[tag]
         g.sync.dma_start(T.wt[:, 512 * a:512 * b], T.w[:, 512 * a:512 * b]).then_inc(S["wl" + tag], 16)
 
     g.sync.dma_start(T.xt[:, :], T.x[:, :]).then_inc(S.xl, 16)
     for k in range(8):
         q = g.sync if k >= 5 else A
         q.dma_start(T.snt[16 * k:16 * k + 16, :], T.sn[:, :]).then_inc(S.snl, 16)
-    load_w("0", 0, 4)
-    A.dma_start(T.vt[:, :], T.v[:, :]).then_inc(S.vl, 16)
-    load_w("1", 4, 8)
-    load_w("2", 8, 12)
-    load_w("3", 12, 14)
-    load_w("3b", 14, 16)
-    for k in range(4):
-        g.sync.dma_start(T.sot[16 * k:16 * k + 16, :], T.so[:, :]).then_inc(S.sol, 16)
+    load_w("0")
+    for k in range(8):
+        A.dma_start(T.sot[16 * k:16 * k + 16, :], T.so[:, :]).then_inc(S.sol, 16)
+    g.sync.wait_ge(S.xl, 16)
+    g.sync.dma_start(T.vt[:, :], T.v[:, :]).then_inc(S.vl, 16)
+    load_w("1")
+    g.sync.wait_ge(S.wl0, 16)
+    load_w("2")
+    g.sync.wait_ge(S.vl, 16)
+    load_w("3")
+    load_w("3b")
 
     V.memset(T.zt[:, :], 0.0).then_inc(S.zm, 1)
     V.wait_ge(S.zm, 1)
@@ -93,10 +97,10 @@ def rank_program(g, core, T, topo):
     V.tensor_copy(T.offs[:, o0:o0 + K], T.snt[:, K * r:K * r + K]).then_inc(S.cvo, 1)
     V.wait_ge(S.cvo, 1)
     V.tensor_copy(u32(T.landq[:, own:own + CAPP]), u32(T.xq[:, :]).indirect(T.offs[:, o0:o0 + K])).then_inc(S.oc, 1)
-    for k in range(4, 8):
-        A.dma_start(T.sot[16 * k:16 * k + 16, :], T.so[:, :]).then_inc(S.sol, 16)
     A.wait_ge(S.cvo, 1)
     A.activation(T.lands[:, own:own + CAPP], T.xs[:, :].indirect(T.offs[:, o0:o0 + K]), COPY).then_inc(S.osc, 1)
+    V.wait_ge(S.sol, 128)
+    V.tensor_scalar(T.offt[:, :], T.sot[:, :], EC, None, AluOpType.add).then_inc(S.cvt, 1)
 
     far, near, plan = 0, 0, []
     for i in range(1, NR):
@@ -131,108 +135,84 @@ def rank_program(g, core, T, topo):
     send(False)
     g.wait_ge(S.loc, 2 * narr)
 
-    def quant_w(tag, a, b):
+    def quant_w(tag):
+        a, b = PIECES[tag]
         V.wait_ge(S["wl" + tag], 16)
         V.quantize_mx(T.wq[:, 128 * a:128 * b], T.ws[:, 128 * a:128 * b], T.wt[:, 512 * a:512 * b]).then_inc(S["wqd" + tag], 1)
 
     def bank(m, b):
         return T["ps%d" % (4 * (m % 2) + b)][:, 0:EC]
 
-    def pick_codes(m):
-        V.tensor_copy(u32(T.tokq[:, EC * m:EC * m + EC]), u32(T.landq[:, :]).indirect(T.offt[:, 8 * m:8 * m + 8])).then_inc(S["pkc%d" % m], 1)
+    def cols(m):
+        return slice(EC * m, EC * m + EC)
 
-    def pick_scales(m):
-        A.activation(T.toks[:, EC * m:EC * m + EC], T.lands[:, :].indirect(T.offt[:, 8 * m:8 * m + 8]), COPY).then_inc(S["pks%d" % m], 1)
-
-    def h_out(m, b):
-        return T.ht[:, 512 * m + b:512 * m + 512:4]
-
-    def evac(m, *bs):
-        for b in bs:
-            if b in ON_SCALAR[m]:
-                A.wait_ge(S["mm%d_%d" % (m, b)], 1)
-                A.activation(h_out(m, b), bank(m, b), RELU, scale=0.05).then_inc(S["ev%d_%d" % (m, b)], 1)
+    def work(q, op):
+        k, m = op[0], int(op[1])
+        done = None if k == "w" else S[op]
+        b = int(op[2]) if k in "me" else 0
+        if k == "w":
+            quant_w(op[1:])
+        elif k == "p":
+            q.tensor_copy(u32(T.tokq[:, cols(m)]), u32(T.landq[:, :]).indirect(T.offt[:, 8 * m:8 * m + 8])).then_inc(done, 1)
+        elif k == "s":
+            src = T.lands[:, :].indirect(T.offt[:, 8 * m:8 * m + 8])
+            if q is A:
+                q.activation(T.toks[:, cols(m)], src, COPY).then_inc(done, 1)
             else:
-                V.wait_ge(S["mm%d_%d" % (m, b)], 1)
-                V.tensor_scalar(h_out(m, b), bank(m, b), 0.0, 0.05, AluOpType.max, AluOpType.mult).then_inc(S["ev%d_%d" % (m, b)], 1)
-
-    def quant_h(m):
-        for b in range(4):
-            V.wait_ge(S["ev%d_%d" % (m, b)], 1)
-        V.quantize_mx(T.hq[:, EC * m:EC * m + EC], T.hs[:, EC * m:EC * m + EC], T.ht[:, 512 * m:512 * m + 512]).then_inc(S["hqd%d" % m], 1)
-
-    def y_out(m):
-        A.wait_ge(S["mv%d" % m], 1)
-        A.activation(T.yt[:, EC * m:EC * m + EC], bank(m, 3), COPY).then_inc(S["ye%d" % m], 1)
-        g.sync.wait_ge(S["ye%d" % m], 1)
-        g.sync.dma_start(T.y[:, EC * m:EC * m + EC], T.yt[:, EC * m:EC * m + EC]).then_inc(S.yd, 16)
-
-    def mm_w(m, *bs):
-        for b in bs:
-            if b == 0:
-                P.wait_ge(S["wqd%d" % m], 1)
-                P.wait_ge(S["pkc%d" % m], 1)
-                P.wait_ge(S["pks%d" % m], 1)
-            if m == 3 and b == 2:
-                P.wait_ge(S.wqd3b, 1)
-            if m >= 2 and b == 3:
-                P.wait_ge(S["ye%d" % (m - 2)], 1)
+                q.tensor_copy(T.toks[:, cols(m)], src).then_inc(done, 1)
+        elif k == "m":
+            q.wait_ge(S["p%d" % m], 1)
+            q.wait_ge(S["s%d" % m], 1)
+            q.wait_ge(S["wqd3b" if m == 3 and b > 1 else "wqd%d" % m], 1)
+            if m >= 2:
+                q.wait_ge(S["e%d%d" % (m - 2, b)], 1)
+                if b == 3:
+                    q.wait_ge(S["y%d" % (m - 2)], 1)
             c = 512 * m + 128 * b
-            P.matmul_mx(bank(m, b), T.wq[:, c:c + 128], T.ws[:, c:c + 128], T.tokq[:, EC * m:EC * m + EC],
-                        T.toks[:, EC * m:EC * m + EC], True, True).then_inc(S["mm%d_%d" % (m, b)], 1)
+            q.matmul_mx(bank(m, b), T.wq[:, c:c + 128], T.ws[:, c:c + 128], T.tokq[:, cols(m)], T.toks[:, cols(m)], True, True).then_inc(done, 1)
+        elif k == "e":
+            q.wait_ge(S["m" + op[1:]], 1)
+            h = T.ht[:, 512 * m + b:512 * m + 512:4]
+            if q is A:
+                q.activation(h, bank(m, b), RELU, scale=0.05).then_inc(done, 1)
+            else:
+                q.tensor_scalar(h, bank(m, b), 0.0, 0.05, AluOpType.max, AluOpType.mult).then_inc(done, 1)
+        elif k == "h":
+            for c in range(4):
+                q.wait_ge(S["e%d%d" % (m, c)], 1)
+            q.quantize_mx(T.hq[:, cols(m)], T.hs[:, cols(m)], T.ht[:, 512 * m:512 * m + 512]).then_inc(done, 1)
+        elif k == "v":
+            q.wait_ge(S.vqd, 1)
+            q.wait_ge(S["h%d" % m], 1)
+            q.matmul_mx(bank(m, 3), T.vq[:, cols(m)], T.vs[:, cols(m)], T.hq[:, cols(m)], T.hs[:, cols(m)], True, True).then_inc(done, 1)
+        elif k == "y":
+            q.wait_ge(S["v%d" % m], 1)
+            if q is A:
+                q.activation(T.yt[:, cols(m)], bank(m, 3), COPY).then_inc(done, 1)
+            else:
+                q.tensor_copy(T.yt[:, cols(m)], bank(m, 3)).then_inc(done, 1)
 
-    def mm_v(m):
-        if m == 0:
-            P.wait_ge(S.vqd, 1)
-        P.wait_ge(S["hqd%d" % m], 1)
-        P.matmul_mx(bank(m, 3), T.vq[:, 128 * m:128 * m + 128], T.vs[:, 128 * m:128 * m + 128], T.hq[:, EC * m:EC * m + EC],
-                    T.hs[:, EC * m:EC * m + EC], True, True).then_inc(S["mv%d" % m], 1)
-
-    mm_w(0, 0, 1, 2, 3)
-    mm_w(1, 0, 1, 2, 3)
-    mm_v(0)
-    mm_w(2, 0, 1, 2, 3)
-    mm_v(1)
-    mm_w(3, 0, 1)
-    mm_v(2)
-    mm_w(3, 2, 3)
-    mm_v(3)
-    quant_w("0", 0, 4)
+    quant_w("0")
     V.wait_ge(S.vl, 16)
     V.quantize_mx(T.vq[:, :], T.vs[:, :], T.vt[:, :]).then_inc(S.vqd, 1)
-    quant_w("1", 4, 8)
-    V.wait_ge(S.sol, 128)
-    V.tensor_scalar(T.offt[:, :], T.sot[:, :], EC, None, AluOpType.add).then_inc(S.cvt, 1)
-    V.wait_ge(S.cvt, 1)
-    V.wait_ge(S.zq, 1)
+    quant_w("1")
+    for q in (V, A):
+        q.wait_ge(S.cvt, 1)
+        q.wait_ge(S.zq, 1)
     V.wait_ge(S.oc, 1)
     V.wait_ge(S.arrc, narr)
-    pick_codes(0)
-    pick_codes(1)
-    A.wait_ge(S.cvt, 1)
-    A.wait_ge(S.zq, 1)
     A.wait_ge(S.osc, 1)
     A.wait_ge(S.arrs, narr)
-    pick_scales(0)
-    pick_scales(1)
-    evac(0, 0, 1, 2, 3)
-    pick_codes(2)
-    pick_scales(2)
-    quant_h(0)
-    y_out(0)
-    quant_w("2", 8, 12)
-    evac(1, 0, 1, 2, 3)
-    pick_codes(3)
-    pick_scales(3)
-    quant_h(1)
-    y_out(1)
-    quant_w("3", 12, 14)
-    evac(2, 0, 1, 2, 3)
-    quant_h(2)
-    quant_w("3b", 14, 16)
-    evac(3, 0, 1)
-    y_out(2)
-    evac(3, 2, 3)
-    quant_h(3)
-    y_out(3)
+    for op in TENSOR:
+        work(P, op)
+    for op in SCALAR:
+        work(A, op)
+    for op in VECTOR:
+        if op == "s1":
+            V.wait_ge(S.osc, 1)
+            V.wait_ge(S.arrs, narr)
+        work(V, op)
+    for m in (0, 1, 2, 3):
+        g.sync.wait_ge(S["y%d" % m], 1)
+        g.sync.dma_start(T.y[:, cols(m)], T.yt[:, cols(m)]).then_inc(S.yd, 16)
     g.sync.wait_ge(S.yd, 16 * E)

@@ -4,10 +4,15 @@ from concourse.mybir import dt, AluOpType, ActivationFunctionType
 E, EC, CAPP, NR, TOK = 4, 128, 48, 8, 256
 F8 = "float8_e4m3fn_x4"
 WIN = EC + NR * CAPP
-TENSOR = "m00 m02 m01 m12 m03 m10 m11 m13 m21 m22 v0 m20 m30 v1 m23 m32 m31 m33 v2 v3".split()
-VECTOR = "p0 p1 p2 s1 w2 e00 e12 p3 h0 w3 e11 h1 w3b e20 y1 e30 h2 e33 h3 y2".split()
-SCALAR = "s0 s2 s3 e02 e01 e03 e10 e13 e21 y0 e22 e23 e32 e31 y3".split()
-PIECES = {"0": (0, 4), "1": (4, 8), "2": (8, 12), "3": (12, 14), "3b": (14, 16)}
+XP = {"0": (0, 128), "1": (128, 256)}
+WP = {"0": (0, 4), "1": (4, 8), "2": (8, 12), "3": (12, 14), "3b": (14, 16)}
+VP = {"a": (0, 2), "b": (2, 4)}
+SYNC = "Lx0 Lx1 Ln5 Ln6 Ln7 Lw0 ?xl1 Lva Lw1 ?wl0 Lw2 ?loc Lw3 Lw3b Lvb".split()
+ACT0 = "Ln0 Ln1 Ln2 Ln3 Ln4 Lo0 Lo1 Lo2 Lo3 Lo4 Lo5 Lo6 Lo7".split()
+VECTOR = "w0 ua w1 ?ready ?arrc p0 p1 ?arrs s1 p23 w2 e12 h0 e11 w3 h1 w3b e30 ub h2 e33 h3 y2 y3".split()
+TENSOR = "m02 m00 m03 m01 m12 m13 m10 m11 m21 m22 v0 m20 m30 v1 m23 m32 m31 m33 v2 v3".split()
+SCALAR = "?ready ?arrs s0 s23 e02 e00 e01 e03 e13 e10 e21 e22 y0 e20 y1 e23 e32 e31".split()
+STORES = (0, 1, 2, 3)
 SCRATCH = {
     "snt": ("sbuf", [128, 24], "int32"),
     "sot": ("sbuf", [128, 32], "int32"),
@@ -36,9 +41,10 @@ SCRATCH = {
 }
 for _i in range(8):
     SCRATCH["ps%d" % _i] = ("psum", [128, 512], "float32")
-SEMAPHORES = ["snl", "xl", "sol", "vl", "zm", "zq", "cv", "cvo", "cvt", "xqd", "pc", "psc", "oc", "osc",
-              "arrc", "arrs", "loc", "vqd", "yd"]
-SEMAPHORES += ["wl" + _t for _t in PIECES] + ["wqd" + _t for _t in PIECES] + sorted(set(TENSOR + VECTOR + SCALAR) - {"w2", "w3", "w3b"})
+PICKS = {_k + _d: _o for _o in VECTOR + SCALAR if _o[0] in "ps" for _k in _o[0] for _d in _o[1:]}
+SEMAPHORES = ["snl", "sol", "zm", "zq", "cv", "cvo", "cvt", "xqd", "pc", "psc", "oc", "osc", "arrc", "arrs", "loc", "yd"]
+SEMAPHORES += ["xl" + _t for _t in XP] + ["wl" + _t for _t in WP] + ["wqd" + _t for _t in WP] + ["vl" + _t for _t in VP] + ["vqd" + _t for _t in VP]
+SEMAPHORES += sorted({_o for _o in TENSOR + VECTOR + SCALAR if _o[0] in "psmehvy"})
 
 
 def rank_program(g, core, T, topo):
@@ -47,30 +53,111 @@ def rank_program(g, core, T, topo):
         return
     S, V, A, P = T.sem, g.vector, g.scalar, g.tensor
     COPY, RELU = ActivationFunctionType.Copy, ActivationFunctionType.Relu
+    narr = 2 * (NR - 1)
 
     def u32(ap):
         return ap.bitcast(dt.uint32)
 
-    def load_w(tag):
-        a, b = PIECES[tag]
-        g.sync.dma_start(T.wt[:, 512 * a:512 * b], T.w[:, 512 * a:512 * b]).then_inc(S["wl" + tag], 16)
+    def bank(m, b):
+        return T["ps%d" % (4 * (m % 2) + b)][:, 0:EC]
 
-    g.sync.dma_start(T.xt[:, :], T.x[:, :]).then_inc(S.xl, 16)
-    for k in range(8):
-        q = g.sync if k >= 5 else A
-        q.dma_start(T.snt[16 * k:16 * k + 16, :], T.sn[:, :]).then_inc(S.snl, 16)
-    load_w("0")
-    for k in range(8):
-        A.dma_start(T.sot[16 * k:16 * k + 16, :], T.so[:, :]).then_inc(S.sol, 16)
-    g.sync.wait_ge(S.xl, 16)
-    g.sync.dma_start(T.vt[:, :], T.v[:, :]).then_inc(S.vl, 16)
-    load_w("1")
-    g.sync.wait_ge(S.wl0, 16)
-    load_w("2")
-    g.sync.wait_ge(S.vl, 16)
-    load_w("3")
-    load_w("3b")
+    def cols(m):
+        return slice(EC * m, EC * m + EC)
 
+    def piece(pieces, i):
+        return [t for t in pieces if pieces[t][0] <= i < pieces[t][1]][0]
+
+    def wait(q, s):
+        if s == "ready":
+            q.wait_ge(S.cvt, 1)
+            q.wait_ge(S.zq, 1)
+            q.wait_ge(S.oc if q is V else S.osc, 1)
+        elif s == "arrs" and q is V:
+            q.wait_ge(S.osc, 1)
+            q.wait_ge(S.arrs, narr)
+        elif s in ("arrc", "arrs"):
+            q.wait_ge(S[s], narr)
+        elif s == "loc":
+            q.wait_ge(S.loc, 2 * narr)
+        else:
+            q.wait_ge(S[s], 128 if s in ("snl", "sol") else 16)
+
+    def load(q, op):
+        k, t = op[0], op[1:]
+        if k == "x":
+            a, b = XP[t]
+            q.dma_start(T.xt[:, 4 * a:4 * b], T.x[:, 4 * a:4 * b]).then_inc(S["xl" + t], 16)
+        elif k in "no":
+            i = int(t)
+            dst, src = (T.snt, T.sn) if k == "n" else (T.sot, T.so)
+            q.dma_start(dst[16 * i:16 * i + 16, :], src[:, :]).then_inc(S.snl if k == "n" else S.sol, 16)
+        elif k == "w":
+            a, b = WP[t]
+            q.dma_start(T.wt[:, 512 * a:512 * b], T.w[:, 512 * a:512 * b]).then_inc(S["wl" + t], 16)
+        elif k == "v":
+            a, b = VP[t]
+            q.dma_start(T.vt[:, 512 * a:512 * b], T.v[:, 512 * a:512 * b]).then_inc(S["vl" + t], 16)
+
+    def work(q, op):
+        k, t = op[0], op[1:]
+        if k == "?":
+            return wait(q, t)
+        if k == "L":
+            return load(q, t)
+        if k in "wu":
+            n = "w" if k == "w" else "v"
+            a, b = (WP if k == "w" else VP)[t]
+            q.wait_ge(S[n + "l" + t], 16)
+            q.quantize_mx(T[n + "q"][:, 128 * a:128 * b], T[n + "s"][:, 128 * a:128 * b], T[n + "t"][:, 512 * a:512 * b]).then_inc(S[n + "qd" + t], 1)
+            return
+        m = int(op[1])
+        b = int(op[2]) if k in "me" else 0
+        done = S[op]
+        if k in "ps":
+            n = len(op) - 1
+            to, off = slice(EC * m, EC * (m + n)), T.offt[:, 8 * m:8 * (m + n)]
+            if k == "p":
+                q.tensor_copy(u32(T.tokq[:, to]), u32(T.landq[:, :]).indirect(off)).then_inc(done, 1)
+            elif q is A:
+                q.activation(T.toks[:, to], T.lands[:, :].indirect(off), COPY).then_inc(done, 1)
+            else:
+                q.tensor_copy(T.toks[:, to], T.lands[:, :].indirect(off)).then_inc(done, 1)
+        elif k == "m":
+            q.wait_ge(S[PICKS["p%d" % m]], 1)
+            q.wait_ge(S[PICKS["s%d" % m]], 1)
+            q.wait_ge(S["wqd" + piece(WP, 4 * m + b)], 1)
+            if m >= 2:
+                q.wait_ge(S["e%d%d" % (m - 2, b)], 1)
+                if b == 3:
+                    q.wait_ge(S["y%d" % (m - 2)], 1)
+            c = 512 * m + 128 * b
+            q.matmul_mx(bank(m, b), T.wq[:, c:c + 128], T.ws[:, c:c + 128], T.tokq[:, cols(m)], T.toks[:, cols(m)], True, True).then_inc(done, 1)
+        elif k == "e":
+            q.wait_ge(S["m" + op[1:]], 1)
+            h = T.ht[:, 512 * m + b:512 * m + 512:4]
+            if q is A:
+                q.activation(h, bank(m, b), RELU, scale=0.05).then_inc(done, 1)
+            else:
+                q.tensor_scalar(h, bank(m, b), 0.0, 0.05, AluOpType.max, AluOpType.mult).then_inc(done, 1)
+        elif k == "h":
+            for c in range(4):
+                q.wait_ge(S["e%d%d" % (m, c)], 1)
+            q.quantize_mx(T.hq[:, cols(m)], T.hs[:, cols(m)], T.ht[:, 512 * m:512 * m + 512]).then_inc(done, 1)
+        elif k == "v":
+            q.wait_ge(S["vqd" + piece(VP, m)], 1)
+            q.wait_ge(S["h%d" % m], 1)
+            q.matmul_mx(bank(m, 3), T.vq[:, cols(m)], T.vs[:, cols(m)], T.hq[:, cols(m)], T.hs[:, cols(m)], True, True).then_inc(done, 1)
+        elif k == "y":
+            q.wait_ge(S["v%d" % m], 1)
+            if q is A:
+                q.activation(T.yt[:, cols(m)], bank(m, 3), COPY).then_inc(done, 1)
+            else:
+                q.tensor_copy(T.yt[:, cols(m)], bank(m, 3)).then_inc(done, 1)
+
+    for op in SYNC:
+        work(g.sync, op)
+    for op in ACT0:
+        work(A, op)
     V.memset(T.zt[:, :], 0.0).then_inc(S.zm, 1)
     V.wait_ge(S.zm, 1)
     V.quantize_mx(T.landq[:, 0:EC], T.lands[:, 0:EC], T.zt[:, :]).then_inc(S.zq, 1)
@@ -83,14 +170,16 @@ def rank_program(g, core, T, topo):
     if r < NR - 1:
         V.tensor_copy(T.offs[:, K * r:K * (NR - 1)], T.snt[:, K * (r + 1):K * NR]).then_inc(S.cv, 1)
         ncv += 1
-    V.wait_ge(S.xl, 16)
-    V.quantize_mx(T.xq[:, :], T.xs[:, :], T.xt[:, :]).then_inc(S.xqd, 1)
+    for t in XP:
+        a, b = XP[t]
+        V.wait_ge(S["xl" + t], 16)
+        V.quantize_mx(T.xq[:, a:b], T.xs[:, a:b], T.xt[:, 4 * a:4 * b]).then_inc(S.xqd, 1)
     V.wait_ge(S.cv, ncv)
-    V.wait_ge(S.xqd, 1)
+    V.wait_ge(S.xqd, len(XP))
     n7 = K * (NR - 1)
     V.tensor_copy(u32(T.slotq[:, :]), u32(T.xq[:, :]).indirect(T.offs[:, 0:n7])).then_inc(S.pc, 1)
     A.wait_ge(S.cv, ncv)
-    A.wait_ge(S.xqd, 1)
+    A.wait_ge(S.xqd, len(XP))
     A.activation(T.slots[:, :], T.xs[:, :].indirect(T.offs[:, 0:n7]), COPY).then_inc(S.psc, 1)
     o0 = n7 + n7 % 2
     own = EC + CAPP * r
@@ -128,91 +217,19 @@ def rank_program(g, core, T, topo):
             ts.append(RemoteDMATransfer(dst_ids=[did], dma_engine_mask=mask, remote_sem=S.arrc if codes else S.arrs, src=src, dst=dst))
         g.remote_dma_fused(ts, local_sem=S.loc)
 
-    narr = 2 * (NR - 1)
     g.wait_ge(S.pc, 1)
     send(True)
     g.wait_ge(S.psc, 1)
     send(False)
     g.wait_ge(S.loc, 2 * narr)
 
-    def quant_w(tag):
-        a, b = PIECES[tag]
-        V.wait_ge(S["wl" + tag], 16)
-        V.quantize_mx(T.wq[:, 128 * a:128 * b], T.ws[:, 128 * a:128 * b], T.wt[:, 512 * a:512 * b]).then_inc(S["wqd" + tag], 1)
-
-    def bank(m, b):
-        return T["ps%d" % (4 * (m % 2) + b)][:, 0:EC]
-
-    def cols(m):
-        return slice(EC * m, EC * m + EC)
-
-    def work(q, op):
-        k, m = op[0], int(op[1])
-        done = None if k == "w" else S[op]
-        b = int(op[2]) if k in "me" else 0
-        if k == "w":
-            quant_w(op[1:])
-        elif k == "p":
-            q.tensor_copy(u32(T.tokq[:, cols(m)]), u32(T.landq[:, :]).indirect(T.offt[:, 8 * m:8 * m + 8])).then_inc(done, 1)
-        elif k == "s":
-            src = T.lands[:, :].indirect(T.offt[:, 8 * m:8 * m + 8])
-            if q is A:
-                q.activation(T.toks[:, cols(m)], src, COPY).then_inc(done, 1)
-            else:
-                q.tensor_copy(T.toks[:, cols(m)], src).then_inc(done, 1)
-        elif k == "m":
-            q.wait_ge(S["p%d" % m], 1)
-            q.wait_ge(S["s%d" % m], 1)
-            q.wait_ge(S["wqd3b" if m == 3 and b > 1 else "wqd%d" % m], 1)
-            if m >= 2:
-                q.wait_ge(S["e%d%d" % (m - 2, b)], 1)
-                if b == 3:
-                    q.wait_ge(S["y%d" % (m - 2)], 1)
-            c = 512 * m + 128 * b
-            q.matmul_mx(bank(m, b), T.wq[:, c:c + 128], T.ws[:, c:c + 128], T.tokq[:, cols(m)], T.toks[:, cols(m)], True, True).then_inc(done, 1)
-        elif k == "e":
-            q.wait_ge(S["m" + op[1:]], 1)
-            h = T.ht[:, 512 * m + b:512 * m + 512:4]
-            if q is A:
-                q.activation(h, bank(m, b), RELU, scale=0.05).then_inc(done, 1)
-            else:
-                q.tensor_scalar(h, bank(m, b), 0.0, 0.05, AluOpType.max, AluOpType.mult).then_inc(done, 1)
-        elif k == "h":
-            for c in range(4):
-                q.wait_ge(S["e%d%d" % (m, c)], 1)
-            q.quantize_mx(T.hq[:, cols(m)], T.hs[:, cols(m)], T.ht[:, 512 * m:512 * m + 512]).then_inc(done, 1)
-        elif k == "v":
-            q.wait_ge(S.vqd, 1)
-            q.wait_ge(S["h%d" % m], 1)
-            q.matmul_mx(bank(m, 3), T.vq[:, cols(m)], T.vs[:, cols(m)], T.hq[:, cols(m)], T.hs[:, cols(m)], True, True).then_inc(done, 1)
-        elif k == "y":
-            q.wait_ge(S["v%d" % m], 1)
-            if q is A:
-                q.activation(T.yt[:, cols(m)], bank(m, 3), COPY).then_inc(done, 1)
-            else:
-                q.tensor_copy(T.yt[:, cols(m)], bank(m, 3)).then_inc(done, 1)
-
-    quant_w("0")
-    V.wait_ge(S.vl, 16)
-    V.quantize_mx(T.vq[:, :], T.vs[:, :], T.vt[:, :]).then_inc(S.vqd, 1)
-    quant_w("1")
-    for q in (V, A):
-        q.wait_ge(S.cvt, 1)
-        q.wait_ge(S.zq, 1)
-    V.wait_ge(S.oc, 1)
-    V.wait_ge(S.arrc, narr)
-    A.wait_ge(S.osc, 1)
-    A.wait_ge(S.arrs, narr)
     for op in TENSOR:
         work(P, op)
     for op in SCALAR:
         work(A, op)
     for op in VECTOR:
-        if op == "s1":
-            V.wait_ge(S.osc, 1)
-            V.wait_ge(S.arrs, narr)
         work(V, op)
-    for m in (0, 1, 2, 3):
+    for m in STORES:
         g.sync.wait_ge(S["y%d" % m], 1)
         g.sync.dma_start(T.y[:, cols(m)], T.yt[:, cols(m)]).then_inc(S.yd, 16)
     g.sync.wait_ge(S.yd, 16 * E)

from concourse.bass import DstId, RemoteDMATransfer
from concourse.mybir import dt, AluOpType, ActivationFunctionType

E, EC, CAPP, NR, TOK = 4, 128, 48, 8, 256
F8 = "float8_e4m3fn_x4"
WIN = EC + NR * CAPP
XP = {"0": (0, 128), "1": (128, 256)}
WP = {"0": (0, 4), "1": (4, 8), "2": (8, 12), "3": (12, 14), "3b": (14, 16)}
VP = {"a": (0, 2), "b": (2, 4)}
SYNC = "Lx0 Lx1 Ln5 Ln6 Ln7 Lw0 ?xl1 Lva Lw1 ?wl0 Lw2 ?loc Lw3 Lw3b Lvb".split()
ACT0 = "Ln0 Ln1 Ln2 Ln3 Ln4 Lo0 Lo1 Lo2 Lo3 Lo4 Lo5 Lo6 Lo7".split()
VECTOR = "w0 ua w1 ?ready ?arrc p0 p1 ?arrs s1 p23 w2 e12 h0 e11 w3 h1 w3b e30 ub h2 e33 h3 y2 y3".split()
TENSOR = "m02 m00 m03 m01 m12 m13 m10 m11 m21 m22 v0 m20 m30 v1 m23 m32 m31 m33 v2 v3".split()
SCALAR = "?ready ?arrs s0 s23 e02 e00 e01 e03 e13 e10 e21 e22 y0 e20 y1 e23 e32 e31".split()
STORES = (0, 1, 2, 3)
SCRATCH = {
    "snt": ("sbuf", [128, 24], "int32"),
    "sot": ("sbuf", [128, 32], "int32"),
    "offs": ("sbuf", [128, 32], "uint16"),
    "offt": ("sbuf", [128, 32], "uint16"),
    "xt": ("sbuf", [128, 4 * TOK], "bfloat16"),
    "xq": ("sbuf", [128, TOK], F8),
    "xs": ("sbuf", [128, TOK], "uint8"),
    "slotq": ("sbuf", [128, (NR - 1) * CAPP], F8),
    "slots": ("sbuf", [128, (NR - 1) * CAPP], "uint8"),
    "zt": ("sbuf", [128, 4 * EC], "bfloat16"),
    "landq": ("sbuf", [128, WIN], F8),
    "lands": ("sbuf", [128, WIN], "uint8"),
    "tokq": ("sbuf", [128, E * EC], F8),
    "toks": ("sbuf", [128, E * EC], "uint8"),
    "wt": ("sbuf", [128, 2048 * E], "bfloat16"),
    "wq": ("sbuf", [128, 512 * E], F8),
    "ws": ("sbuf", [128, 512 * E], "uint8"),
    "vt": ("sbuf", [128, 512 * E], "bfloat16"),
    "vq": ("sbuf", [128, 128 * E], F8),
    "vs": ("sbuf", [128, 128 * E], "uint8"),
    "ht": ("sbuf", [128, 4 * EC * E], "bfloat16"),
    "hq": ("sbuf", [128, EC * E], F8),
    "hs": ("sbuf", [128, EC * E], "uint8"),
    "yt": ("sbuf", [128, EC * E], "float32"),
}
for _i in range(8):
    SCRATCH["ps%d" % _i] = ("psum", [128, 512], "float32")
PICKS = {_k + _d: _o for _o in VECTOR + SCALAR if _o[0] in "ps" for _k in _o[0] for _d in _o[1:]}
SEMAPHORES = ["snl", "sol", "zm", "zq", "cv", "cvo", "cvt", "xqd", "pc", "psc", "oc", "osc", "arrc", "arrs", "loc", "yd"]
SEMAPHORES += ["xl" + _t for _t in XP] + ["wl" + _t for _t in WP] + ["wqd" + _t for _t in WP] + ["vl" + _t for _t in VP] + ["vqd" + _t for _t in VP]
SEMAPHORES += sorted({_o for _o in TENSOR + VECTOR + SCALAR if _o[0] in "psmehvy"})


def rank_program(g, core, T, topo):
    r = T.rank_of(core)
    if r is None:
        return
    S, V, A, P = T.sem, g.vector, g.scalar, g.tensor
    COPY, RELU = ActivationFunctionType.Copy, ActivationFunctionType.Relu
    narr = 2 * (NR - 1)

    def u32(ap):
        return ap.bitcast(dt.uint32)

    def bank(m, b):
        return T["ps%d" % (4 * (m % 2) + b)][:, 0:EC]

    def cols(m):
        return slice(EC * m, EC * m + EC)

    def piece(pieces, i):
        return [t for t in pieces if pieces[t][0] <= i < pieces[t][1]][0]

    def wait(q, s):
        if s == "ready":
            q.wait_ge(S.cvt, 1)
            q.wait_ge(S.zq, 1)
            q.wait_ge(S.oc if q is V else S.osc, 1)
        elif s == "arrs" and q is V:
            q.wait_ge(S.osc, 1)
            q.wait_ge(S.arrs, narr)
        elif s in ("arrc", "arrs"):
            q.wait_ge(S[s], narr)
        elif s == "loc":
            q.wait_ge(S.loc, 2 * narr)
        else:
            q.wait_ge(S[s], 128 if s in ("snl", "sol") else 16)

    def load(q, op):
        k, t = op[0], op[1:]
        if k == "x":
            a, b = XP[t]
            q.dma_start(T.xt[:, 4 * a:4 * b], T.x[:, 4 * a:4 * b]).then_inc(S["xl" + t], 16)
        elif k in "no":
            i = int(t)
            dst, src = (T.snt, T.sn) if k == "n" else (T.sot, T.so)
            q.dma_start(dst[16 * i:16 * i + 16, :], src[:, :]).then_inc(S.snl if k == "n" else S.sol, 16)
        elif k == "w":
            a, b = WP[t]
            q.dma_start(T.wt[:, 512 * a:512 * b], T.w[:, 512 * a:512 * b]).then_inc(S["wl" + t], 16)
        elif k == "v":
            a, b = VP[t]
            q.dma_start(T.vt[:, 512 * a:512 * b], T.v[:, 512 * a:512 * b]).then_inc(S["vl" + t], 16)

    def work(q, op):
        k, t = op[0], op[1:]
        if k == "?":
            return wait(q, t)
        if k == "L":
            return load(q, t)
        if k in "wu":
            n = "w" if k == "w" else "v"
            a, b = (WP if k == "w" else VP)[t]
            q.wait_ge(S[n + "l" + t], 16)
            q.quantize_mx(T[n + "q"][:, 128 * a:128 * b], T[n + "s"][:, 128 * a:128 * b], T[n + "t"][:, 512 * a:512 * b]).then_inc(S[n + "qd" + t], 1)
            return
        m = int(op[1])
        b = int(op[2]) if k in "me" else 0
        done = S[op]
        if k in "ps":
            n = len(op) - 1
            to, off = slice(EC * m, EC * (m + n)), T.offt[:, 8 * m:8 * (m + n)]
            if k == "p":
                q.tensor_copy(u32(T.tokq[:, to]), u32(T.landq[:, :]).indirect(off)).then_inc(done, 1)
            elif q is A:
                q.activation(T.toks[:, to], T.lands[:, :].indirect(off), COPY).then_inc(done, 1)
            else:
                q.tensor_copy(T.toks[:, to], T.lands[:, :].indirect(off)).then_inc(done, 1)
        elif k == "m":
            q.wait_ge(S[PICKS["p%d" % m]], 1)
            q.wait_ge(S[PICKS["s%d" % m]], 1)
            q.wait_ge(S["wqd" + piece(WP, 4 * m + b)], 1)
            if m >= 2:
                q.wait_ge(S["e%d%d" % (m - 2, b)], 1)
                if b == 3:
                    q.wait_ge(S["y%d" % (m - 2)], 1)
            c = 512 * m + 128 * b
            q.matmul_mx(bank(m, b), T.wq[:, c:c + 128], T.ws[:, c:c + 128], T.tokq[:, cols(m)], T.toks[:, cols(m)], True, True).then_inc(done, 1)
        elif k == "e":
            q.wait_ge(S["m" + op[1:]], 1)
            h = T.ht[:, 512 * m + b:512 * m + 512:4]
            if q is A:
                q.activation(h, bank(m, b), RELU, scale=0.05).then_inc(done, 1)
            else:
                q.tensor_scalar(h, bank(m, b), 0.0, 0.05, AluOpType.max, AluOpType.mult).then_inc(done, 1)
        elif k == "h":
            for c in range(4):
                q.wait_ge(S["e%d%d" % (m, c)], 1)
            q.quantize_mx(T.hq[:, cols(m)], T.hs[:, cols(m)], T.ht[:, 512 * m:512 * m + 512]).then_inc(done, 1)
        elif k == "v":
            q.wait_ge(S["vqd" + piece(VP, m)], 1)
            q.wait_ge(S["h%d" % m], 1)
            q.matmul_mx(bank(m, 3), T.vq[:, cols(m)], T.vs[:, cols(m)], T.hq[:, cols(m)], T.hs[:, cols(m)], True, True).then_inc(done, 1)
        elif k == "y":
            q.wait_ge(S["v%d" % m], 1)
            if q is A:
                q.activation(T.yt[:, cols(m)], bank(m, 3), COPY).then_inc(done, 1)
            else:
                q.tensor_copy(T.yt[:, cols(m)], bank(m, 3)).then_inc(done, 1)

    for op in SYNC:
        work(g.sync, op)
    for op in ACT0:
        work(A, op)
    V.memset(T.zt[:, :], 0.0).then_inc(S.zm, 1)
    V.wait_ge(S.zm, 1)
    V.quantize_mx(T.landq[:, 0:EC], T.lands[:, 0:EC], T.zt[:, :]).then_inc(S.zq, 1)
    K = CAPP // 16
    ncv = 0
    V.wait_ge(S.snl, 128)
    if r > 0:
        V.tensor_copy(T.offs[:, 0:K * r], T.snt[:, 0:K * r]).then_inc(S.cv, 1)
        ncv += 1
    if r < NR - 1:
        V.tensor_copy(T.offs[:, K * r:K * (NR - 1)], T.snt[:, K * (r + 1):K * NR]).then_inc(S.cv, 1)
        ncv += 1
    for t in XP:
        a, b = XP[t]
        V.wait_ge(S["xl" + t], 16)
        V.quantize_mx(T.xq[:, a:b], T.xs[:, a:b], T.xt[:, 4 * a:4 * b]).then_inc(S.xqd, 1)
    V.wait_ge(S.cv, ncv)
    V.wait_ge(S.xqd, len(XP))
    n7 = K * (NR - 1)
    V.tensor_copy(u32(T.slotq[:, :]), u32(T.xq[:, :]).indirect(T.offs[:, 0:n7])).then_inc(S.pc, 1)
    A.wait_ge(S.cv, ncv)
    A.wait_ge(S.xqd, len(XP))
    A.activation(T.slots[:, :], T.xs[:, :].indirect(T.offs[:, 0:n7]), COPY).then_inc(S.psc, 1)
    o0 = n7 + n7 % 2
    own = EC + CAPP * r
    V.tensor_copy(T.offs[:, o0:o0 + K], T.snt[:, K * r:K * r + K]).then_inc(S.cvo, 1)
    V.wait_ge(S.cvo, 1)
    V.tensor_copy(u32(T.landq[:, own:own + CAPP]), u32(T.xq[:, :]).indirect(T.offs[:, o0:o0 + K])).then_inc(S.oc, 1)
    A.wait_ge(S.cvo, 1)
    A.activation(T.lands[:, own:own + CAPP], T.xs[:, :].indirect(T.offs[:, o0:o0 + K]), COPY).then_inc(S.osc, 1)
    V.wait_ge(S.sol, 128)
    V.tensor_scalar(T.offt[:, :], T.sot[:, :], EC, None, AluOpType.add).then_inc(S.cvt, 1)

    far, near, plan = 0, 0, []
    for i in range(1, NR):
        d = (r + i) % NR
        dst = T.cores[d]
        e = topo.engines(core, dst)
        if topo.die(dst) != topo.die(core):
            use = e[0::2][2 * far:2 * far + 2]
            far += 1
        else:
            use = e[1::2][2 * near:2 * near + 2]
            near += 1
        rid, pid, _ = topo.addr(dst)
        plan.append((d if d < r else d - 1, DstId(rid=rid, pnc=pid), sum(1 << k for k in use)))

    def send(codes):
        ts = []
        for j, did, mask in plan:
            if codes:
                src = T.slotq[:, CAPP * j:CAPP * j + CAPP].bitcast(dt.uint8)
                dst = T.landq[:, own:own + CAPP].bitcast(dt.uint8)
            else:
                src = T.slots[:, CAPP * j:CAPP * j + CAPP]
                dst = T.lands[:, own:own + CAPP]
            ts.append(RemoteDMATransfer(dst_ids=[did], dma_engine_mask=mask, remote_sem=S.arrc if codes else S.arrs, src=src, dst=dst))
        g.remote_dma_fused(ts, local_sem=S.loc)

    g.wait_ge(S.pc, 1)
    send(True)
    g.wait_ge(S.psc, 1)
    send(False)
    g.wait_ge(S.loc, 2 * narr)

    for op in TENSOR:
        work(P, op)
    for op in SCALAR:
        work(A, op)
    for op in VECTOR:
        work(V, op)
    for m in STORES:
        g.sync.wait_ge(S["y%d" % m], 1)
        g.sync.dma_start(T.y[:, cols(m)], T.yt[:, cols(m)]).then_inc(S.yd, 16)
    g.sync.wait_ge(S.yd, 16 * E)
